import numpy as np
import ml_dtypes


def mxq(x, axis, fmt="e4m3"):
    dtype, down = {"e4m3": (ml_dtypes.float8_e4m3fn, 7), "e5m2": (ml_dtypes.float8_e5m2, 14)}[fmt]
    v = np.moveaxis(np.asarray(x, np.float32).astype(ml_dtypes.bfloat16).astype(np.float64), axis, -1)
    blocks = v.reshape(v.shape[:-1] + (-1, 32))
    amax = np.abs(blocks).max(-1, keepdims=True)
    byte = np.maximum(np.where(amax > 0, np.frexp(amax)[1] - 1 + 127, 0) - down, 1)
    scale = np.exp2(byte - 127.0)
    codes = (blocks / scale).astype(np.float32).astype(dtype).astype(np.float64)
    return np.moveaxis((codes * scale).reshape(v.shape), -1, axis)


WIDE = False


def mx_kscale(k):
    if not WIDE:
        return np.ones(k)
    levels = np.array([10, -10, 5, -5, 0])
    if k % 512:
        return np.exp2(np.random.permutation(np.resize(levels, k // 32))).repeat(32)
    a = np.empty((k // 512, 16))
    for p in range(k // 512):
        a[p, :8] = np.random.permutation(np.resize(levels, 8))
        for g in range(8):
            far = levels[np.abs(levels - a[p, g]) >= 10]
            a[p, g + 8] = far[np.random.randint(len(far))]
    return np.exp2(a.ravel()).repeat(32)


def f64(x):
    return np.asarray(x).astype(np.float64)


def striped(idx):
    return np.tile(np.asarray(idx).reshape(-1, 16).T, (8, 1)).astype(np.uint16)


def unstriped(offs):
    return offs[:16].T.reshape(-1).astype(np.int64)


B, N, T, D, DV, NQ = 1, 512, 2048, 512, 0, 384


def setup_inputs():
    n = np.random.standard_normal
    idx = np.random.permutation(T)[:B * N]
    s = mx_kscale(D)[:, None]
    return {
        "qT": (n((B, D, NQ)) * s * (1.00 / np.sqrt(D))).astype(np.float32),
        "kT": (n((D, T)) / s).astype(np.float32),
        "kb": np.tile(n(T), (128, 1)).astype(np.float32),
        "offs": striped(idx),
    }


def reference(qT, kT, kb, offs):
    idx = unstriped(offs)
    pick = lambda x: x[:, idx].reshape(x.shape[0], B, N).transpose(1, 0, 2)
    a = mxq(f64(qT), 1, "e4m3").transpose(0, 2, 1) @ mxq(pick(f64(kT)), 1, "e4m3")
    a = a + pick(f64(kb))[:, :1, :]
    out = np.zeros((B, NQ, T))
    for b in range(B):
        out[b][:, idx[b * N:(b + 1) * N]] = a[b]
    return out

@@ -1,0 +1,124 @@
+import concourse.mybir as mybir
+from concourse.masks import make_identity
+
+D, T, N, NQ = 512, 2048, 512, 384
+P = 128
+PACK = 4
+H = N // 2
+
+F32 = mybir.dt.float32
+BF16 = mybir.dt.bfloat16
+U32 = mybir.dt.uint32
+U16 = mybir.dt.uint16
+U8 = mybir.dt.uint8
+FP8X4 = mybir.dt.float8_e4m3fn_x4
+
+FLOPS = 2 * NQ * N * D
+BYTES = 4 * (D * NQ + D * T + T + NQ * T) + 2 * P * (N // 16)
+
+
+def tile_attend_sddmm_kb_kernel(tc, qT, kT, kb, offs, out):
+    nc = tc.nc
+    add = mybir.AluOpType.add
+    with (
+        tc.tile_pool(name="keep", bufs=1) as keep,
+        tc.psum_pool(name="psum", bufs=1) as psum,
+    ):
+        kb_part = keep.tile([P, T // P], F32, name="kb_part")
+        nc.sync.dma_start(out=kb_part[:], in_=kb[0].rearrange("(p c) -> p c", c=T // P))
+        offsets = keep.tile([P, N // 16], U16, name="offsets")
+        nc.sync.dma_start(offsets[:], offs)
+
+        k_rows = kT.rearrange("(p t) n -> p t n", t=PACK)
+        planes = []
+        for t in range(PACK):
+            plane = keep.tile([P, T], F32, name=f"plane{t}")
+            nc.sync.dma_start(out=plane[:], in_=k_rows[:, t, :])
+            planes.append(plane)
+        q_rows = qT[0].rearrange("(p t) q -> p t q", t=PACK)
+        q_raw0 = keep.tile([P, PACK, P], F32, name="q_raw0")
+        nc.sync.dma_start(out=q_raw0[:], in_=q_rows[:, :, 0:P])
+        q_raw1 = keep.tile([P, PACK, NQ - P], F32, name="q_raw1")
+        nc.sync.dma_start(out=q_raw1[:], in_=q_rows[:, :, P:NQ])
+
+        ident = keep.tile([P, P], F32, name="ident")
+        make_identity(nc, ident[:])
+        windows = []
+        for m in range(3):
+            window = keep.tile([P, T], F32, name=f"window{m}")
+            windows.append(window)
+        nc.vector.memset(windows[1][:, 0 : T // 2], 0.0)
+        nc.vector.memset(windows[2][:], 0.0)
+        nc.gpsimd.memset(windows[0][:, 0:P], 0.0)
+        nc.gpsimd.memset(windows[0][:, P : 2 * P], 0.0)
+        nc.gpsimd.memset(windows[0][:, 2 * P : T], 0.0)
+        nc.gpsimd.memset(windows[1][:, T // 2 : T], 0.0)
+
+        kb_pool = keep.tile([P, T], F32, name="kb_pool")
+        kb_view = kb_pool[:].rearrange("q (p c) -> q p c", c=T // P)
+        for b in range(4):
+            bank = psum.tile([P, 4, P], F32, name=f"bank{b}")
+            for j in range(4):
+                c = 4 * b + j
+                nc.tensor.transpose(bank[:, j, :], kb_part[:, c : c + 1].to_broadcast([P, P]), ident[:])
+            nc.scalar.copy(out=kb_view[:, :, 4 * b : 4 * b + 4], in_=bank[:].rearrange("q c p -> q p c"))
+
+        K0 = P
+        Q1 = P + N
+        W = N + NQ
+        grouped = keep.tile([P, W, PACK], BF16, name="grouped", align_bytes=64)
+        codes = keep.tile([P, W], U32, name="codes", align_bytes=64)
+        scales = keep.tile([P, W], U8, name="scales", align_bytes=64)
+        keys = grouped[:, K0:Q1, :]
+
+        kb_listed = keep.tile([P, N], F32, name="kb_listed")
+        nc.vector.tensor_copy(keys[:, :, 0], planes[0][:].indirect(offsets[:]))
+        nc.vector.tensor_copy(kb_listed[:], kb_pool[:].indirect(offsets[:]))
+        nc.vector.tensor_copy(keys[:, 0, 1:4], kb_listed[:, 0:3])
+        for t in range(1, PACK):
+            nc.vector.tensor_copy(keys[:, :, t], planes[t][:].indirect(offsets[:]))
+
+        nc.scalar.copy(out=grouped[:, 0:K0, :], in_=q_raw0[:].rearrange("p t q -> p q t"))
+        for m in range(2):
+            nc.scalar.copy(
+                out=grouped[:, Q1 + m * P : Q1 + (m + 1) * P, :],
+                in_=q_raw1[:, :, m * P : (m + 1) * P].rearrange("p t q -> p q t"),
+            )
+
+        def quantize(start, width):
+            cols = slice(start, start + width)
+            nc.vector.quantize_mx(
+                out=codes[:, cols].bitcast(FP8X4),
+                scales=scales[:, cols],
+                in_=grouped[:, cols, :].rearrange("p n t -> p (n t)"),
+            )
+
+        quantize(0, 2 * P)
+        quantize(2 * P, 2 * P)
+        quantize(4 * P, P)
+        bytes_of = codes[:].bitcast(U8)
+        nc.vector.tensor_copy(bytes_of[:, 4 * Q1 : 4 * Q1 + 4], bytes_of[:, 4 * Q1 - 4 : 4 * Q1])
+        quantize(Q1, 2 * P)
+
+        for m in range(3):
+            q_start = 0 if m == 0 else Q1 + (m - 1) * P
+            q_cols = slice(q_start, q_start + P)
+            acc = psum.tile([P, N], F32, name=f"acc{m}")
+            nc.tensor.matmul_mx(
+                out=acc[:],
+                lhsT=codes[:, q_cols].bitcast(FP8X4),
+                lhsT_scale=scales[:, q_cols],
+                rhs=codes[:, K0:Q1].bitcast(FP8X4),
+                rhs_scale=scales[:, K0:Q1],
+                start=True,
+                stop=True,
+            )
+            score = keep.tile([P, N], F32, name=f"score{m}")
+            if m == 0:
+                nc.vector.tensor_tensor(score[:], acc[:], kb_listed[:], add)
+            else:
+                raw = keep.tile([P, N], F32, name=f"raw{m}")
+                nc.scalar.copy(out=raw[:], in_=acc[:])
+                nc.gpsimd.tensor_tensor(score[:], raw[:], kb_listed[:], add)
+            nc.vector.tensor_copy(windows[m][:].indirect(offsets[:]), score[:])
+            nc.sync.dma_start(out=out[0, m * P : (m + 1) * P, :], in_=windows[m][:])

@@ -27,7 +27,6 @@ def tile_attend_sddmm_kb_kernel(tc, qT, kT, kb, offs, out):
         kb_part = keep.tile([P, T // P], F32, name="kb_part")
         nc.sync.dma_start(out=kb_part[:], in_=kb[0].rearrange("(p c) -> p c", c=T // P))
         offsets = keep.tile([P, N // 16], U16, name="offsets")
-        nc.sync.dma_start(offsets[:], offs)
 
         k_rows = kT.rearrange("(p t) n -> p t n", t=PACK)
         planes = []
@@ -35,11 +34,17 @@ def tile_attend_sddmm_kb_kernel(tc, qT, kT, kb, offs, out):
             plane = keep.tile([P, T], F32, name=f"plane{t}")
             nc.sync.dma_start(out=plane[:], in_=k_rows[:, t, :])
             planes.append(plane)
+            if t == 0:
+                nc.sync.dma_start(offsets[:], offs)
         q_rows = qT[0].rearrange("(p t) q -> p t q", t=PACK)
-        q_raw0 = keep.tile([P, PACK, P], F32, name="q_raw0")
-        nc.sync.dma_start(out=q_raw0[:], in_=q_rows[:, :, 0:P])
-        q_raw1 = keep.tile([P, PACK, NQ - P], F32, name="q_raw1")
-        nc.sync.dma_start(out=q_raw1[:], in_=q_rows[:, :, P:NQ])
+        q_first = keep.tile([P, PACK * P], F32, name="q_first", align_bytes=64)
+        nc.sync.dma_start(out=q_first[:].rearrange("p (t q) -> p t q", t=PACK), in_=q_rows[:, :, 0:P])
+        q_rest = keep.tile([P, PACK * NQ], F32, name="q_rest", align_bytes=64)
+        rest_rows = q_rest[:].rearrange("p (t q) -> p t q", t=PACK)
+        q_raw = [q_first[:].rearrange("p (t q) -> p t q", t=PACK)]
+        for m in (1, 2):
+            q_raw.append(rest_rows[:, :, m * P : (m + 1) * P])
+            nc.sync.dma_start(out=q_raw[m], in_=q_rows[:, :, m * P : (m + 1) * P])
 
         ident = keep.tile([P, P], F32, name="ident")
         make_identity(nc, ident[:])
@@ -57,68 +62,80 @@ def tile_attend_sddmm_kb_kernel(tc, qT, kT, kb, offs, out):
         kb_pool = keep.tile([P, T], F32, name="kb_pool")
         kb_view = kb_pool[:].rearrange("q (p c) -> q p c", c=T // P)
         for b in range(4):
-            bank = psum.tile([P, 4, P], F32, name=f"bank{b}")
+            bank = psum.tile([P, 4, P], F32, name=f"bank{b}", tag=f"bank{b}")
             for j in range(4):
                 c = 4 * b + j
                 nc.tensor.transpose(bank[:, j, :], kb_part[:, c : c + 1].to_broadcast([P, P]), ident[:])
             nc.scalar.copy(out=kb_view[:, :, 4 * b : 4 * b + 4], in_=bank[:].rearrange("q c p -> q p c"))
 
-        K0 = P
-        Q1 = P + N
-        W = N + NQ
-        grouped = keep.tile([P, W, PACK], BF16, name="grouped", align_bytes=64)
-        codes = keep.tile([P, W], U32, name="codes", align_bytes=64)
-        scales = keep.tile([P, W], U8, name="scales", align_bytes=64)
-        keys = grouped[:, K0:Q1, :]
+        stage = keep.tile([P, 8 * P * PACK], BF16, name="stage", align_bytes=64)
+        runs = stage[:].rearrange("p (r n t) -> p r n t", n=P, t=PACK)
+        kb_listed = stage[:, P * PACK : 3 * P * PACK].bitcast(F32)
+        widths = {"first": H, "second": H, 0: P, 1: P, 2: P}
+        codes = {k: keep.tile([P, w], U32, name=f"codes_{k}", align_bytes=64) for k, w in widths.items()}
+        scales = {k: keep.tile([P, w], U8, name=f"scales_{k}", align_bytes=64) for k, w in widths.items()}
 
-        kb_listed = keep.tile([P, N], F32, name="kb_listed")
-        nc.vector.tensor_copy(keys[:, :, 0], planes[0][:].indirect(offsets[:]))
-        nc.vector.tensor_copy(kb_listed[:], kb_pool[:].indirect(offsets[:]))
-        nc.vector.tensor_copy(keys[:, 0, 1:4], kb_listed[:, 0:3])
-        for t in range(1, PACK):
-            nc.vector.tensor_copy(keys[:, :, t], planes[t][:].indirect(offsets[:]))
+        by_half = stage[:].rearrange("p (h r n t) -> p h r n t", h=2, n=P, t=PACK)[:, :, 0:4:3, :, :]
 
-        nc.scalar.copy(out=grouped[:, 0:K0, :], in_=q_raw0[:].rearrange("p t q -> p q t"))
-        for m in range(2):
-            nc.scalar.copy(
-                out=grouped[:, Q1 + m * P : Q1 + (m + 1) * P, :],
-                in_=q_raw1[:, :, m * P : (m + 1) * P].rearrange("p t q -> p q t"),
-            )
+        def gather(t, first, last):
+            listed = offsets[:, first * H // 16 : last * H // 16]
+            nc.vector.tensor_copy(by_half[:, first:last, :, :, t], planes[t][:].indirect(listed))
 
-        def quantize(start, width):
+        def quantize(source, key, start, width):
             cols = slice(start, start + width)
             nc.vector.quantize_mx(
-                out=codes[:, cols].bitcast(FP8X4),
-                scales=scales[:, cols],
-                in_=grouped[:, cols, :].rearrange("p n t -> p (n t)"),
+                out=codes[key][:, cols].bitcast(FP8X4),
+                scales=scales[key][:, cols],
+                in_=source.rearrange("p n t -> p (n t)"),
             )
 
-        quantize(0, 2 * P)
-        quantize(2 * P, 2 * P)
-        quantize(4 * P, P)
-        bytes_of = codes[:].bitcast(U8)
-        nc.vector.tensor_copy(bytes_of[:, 4 * Q1 : 4 * Q1 + 4], bytes_of[:, 4 * Q1 - 4 : 4 * Q1])
-        quantize(Q1, 2 * P)
+        def queries(m, target):
+            nc.scalar.copy(out=target, in_=q_raw[m].rearrange("p t q -> p q t"))
+            quantize(target, m, 0, P)
 
-        for m in range(3):
-            q_start = 0 if m == 0 else Q1 + (m - 1) * P
-            q_cols = slice(q_start, q_start + P)
-            acc = psum.tile([P, N], F32, name=f"acc{m}")
-            nc.tensor.matmul_mx(
-                out=acc[:],
-                lhsT=codes[:, q_cols].bitcast(FP8X4),
-                lhsT_scale=scales[:, q_cols],
-                rhs=codes[:, K0:Q1].bitcast(FP8X4),
-                rhs_scale=scales[:, K0:Q1],
-                start=True,
-                stop=True,
-            )
-            score = keep.tile([P, N], F32, name=f"score{m}")
-            if m == 0:
-                nc.vector.tensor_tensor(score[:], acc[:], kb_listed[:], add)
-            else:
-                raw = keep.tile([P, N], F32, name=f"raw{m}")
-                nc.scalar.copy(out=raw[:], in_=acc[:])
-                nc.gpsimd.tensor_tensor(score[:], raw[:], kb_listed[:], add)
-            nc.vector.tensor_copy(windows[m][:].indirect(offsets[:]), score[:])
+        def multiply(m, start, width, tag):
+            acc = psum.tile([P, width], F32, name=f"acc{m}_{start}", tag=tag)
+            for col in range(0, width, H):
+                half = "first" if start + col < H else "second"
+                nc.tensor.matmul_mx(
+                    out=acc[:, col : col + H],
+                    lhsT=codes[m][:].bitcast(FP8X4),
+                    lhsT_scale=scales[m][:],
+                    rhs=codes[half][:].bitcast(FP8X4),
+                    rhs_scale=scales[half][:],
+                    start=True,
+                    stop=True,
+                )
+            return acc
+
+        def scatter(m, start, width, raw):
+            listed = offsets[:, start // 16 : (start + width) // 16]
+            nc.vector.tensor_tensor(windows[m][:].indirect(listed), raw, kb_listed[:, start : start + width], add)
+
+        def scores(m, start, width, tag, raw):
+            nc.scalar.copy(out=raw, in_=multiply(m, start, width, tag)[:])
+            scatter(m, start, width, raw)
+
+        for t in range(PACK - 1):
+            gather(t, 0, 2)
+            if t == 0:
+                nc.vector.tensor_copy(kb_listed, kb_pool[:].indirect(offsets[:]))
+        gather(3, 0, 1)
+        quantize(runs[:, 0], "first", 0, P)
+        quantize(runs[:, 3], "first", P, P)
+        queries(0, runs[:, 5])
+        gather(3, 1, 2)
+        queries(1, q_first[:, 0:H].bitcast(BF16).rearrange("p (q t) -> p q t", t=PACK))
+        acc = multiply(0, 0, H, "acc0")
+        first_raw = q_rest[:, NQ : NQ + H]
+        nc.scalar.copy(out=first_raw, in_=acc[:])
+        quantize(runs[:, 4], "second", 0, P)
+        quantize(runs[:, 7], "second", P, P)
+        scatter(0, 0, H, first_raw)
+        queries(2, q_first[:, H:N].bitcast(BF16).rearrange("p (q t) -> p q t", t=PACK))
+        scores(0, H, H, "acc1", q_rest[:, 3 * NQ - P : 3 * NQ + P])
+        nc.sync.dma_start(out=out[0, 0:P, :], in_=windows[0][:])
+        for m in (1, 2):
+            raw = keep.tile([P, N], F32, name=f"raw{m}")
+            scores(m, 0, N, f"acc{m + 1}", raw[:])
             nc.sync.dma_start(out=out[0, m * P : (m + 1) * P, :], in_=windows[m][:])

@@ -73,7 +73,8 @@ def tile_attend_sddmm_kb_kernel(tc, qT, kT, kb, offs, out):
         kb_listed = stage[:, P * PACK : 3 * P * PACK].bitcast(F32)
         widths = {"first": H, "second": H, 0: P, 1: P, 2: P}
         codes = {k: keep.tile([P, w], U32, name=f"codes_{k}", align_bytes=64) for k, w in widths.items()}
-        scales = {k: keep.tile([P, w], U8, name=f"scales_{k}", align_bytes=64) for k, w in widths.items()}
+        scales = {k: keep.tile([P, w], U8, name=f"scales_{k}", align_bytes=64)[:] for k, w in widths.items() if k != 2}
+        scales[2] = scales[0][4:P, :]
 
         by_half = stage[:].rearrange("p (h r n t) -> p h r n t", h=2, n=P, t=PACK)[:, :, 0:4:3, :, :]
 
@@ -89,8 +90,11 @@ def tile_attend_sddmm_kb_kernel(tc, qT, kT, kb, offs, out):
                 in_=source.rearrange("p n t -> p (n t)"),
             )
 
-        def queries(m, target):
+        def lay_out(m, target):
             nc.scalar.copy(out=target, in_=q_raw[m].rearrange("p t q -> p q t"))
+
+        def queries(m, target):
+            lay_out(m, target)
             quantize(target, m, 0, P)
 
         def multiply(m, start, width, tag):
@@ -100,9 +104,9 @@ def tile_attend_sddmm_kb_kernel(tc, qT, kT, kb, offs, out):
                 nc.tensor.matmul_mx(
                     out=acc[:, col : col + H],
                     lhsT=codes[m][:].bitcast(FP8X4),
-                    lhsT_scale=scales[m][:],
+                    lhsT_scale=scales[m],
                     rhs=codes[half][:].bitcast(FP8X4),
-                    rhs_scale=scales[half][:],
+                    rhs_scale=scales[half],
                     start=True,
                     stop=True,
                 )
@@ -125,15 +129,20 @@ def tile_attend_sddmm_kb_kernel(tc, qT, kT, kb, offs, out):
         quantize(runs[:, 3], "first", P, P)
         queries(0, runs[:, 5])
         gather(3, 1, 2)
-        queries(1, q_first[:, 0:H].bitcast(BF16).rearrange("p (q t) -> p q t", t=PACK))
+        q_staged = q_first[:, 0:H].bitcast(BF16).rearrange("p (q t) -> p q t", t=PACK)
+        queries(1, q_staged)
         acc = multiply(0, 0, H, "acc0")
         first_raw = q_rest[:, NQ : NQ + H]
         nc.scalar.copy(out=first_raw, in_=acc[:])
         quantize(runs[:, 4], "second", 0, P)
         quantize(runs[:, 7], "second", P, P)
         scatter(0, 0, H, first_raw)
-        queries(2, q_first[:, H:N].bitcast(BF16).rearrange("p (q t) -> p q t", t=PACK))
-        scores(0, H, H, "acc1", q_rest[:, 3 * NQ - P : 3 * NQ + P])
+        lay_out(2, q_staged)
+        acc = multiply(0, H, H, "acc1")
+        quantize(q_staged, 2, 0, P)
+        second_raw = q_rest[:, 3 * NQ - P : 3 * NQ + P]
+        nc.scalar.copy(out=second_raw, in_=acc[:])
+        scatter(0, H, H, second_raw)
         nc.sync.dma_start(out=out[0, 0:P, :], in_=windows[0][:])
         for m in (1, 2):
             raw = keep.tile([P, N], F32, name=f"raw{m}")

@@ -91,7 +91,10 @@ def tile_attend_sddmm_kb_kernel(tc, qT, kT, kb, offs, out):
             )
 
         def lay_out(m, target):
-            nc.scalar.copy(out=target, in_=q_raw[m].rearrange("p t q -> p q t"))
+            nc.scalar.copy(
+                out=target.rearrange("p (c i) t -> p c t i", i=4),
+                in_=q_raw[m].rearrange("p t (c i) -> p c t i", i=4),
+            )
 
         def queries(m, target):
             lay_out(m, target)

@@ -37,7 +37,7 @@ def tile_attend_sddmm_kb_kernel(tc, qT, kT, kb, offs, out):
             if t == 0:
                 nc.sync.dma_start(offsets[:], offs)
         q_rows = qT[0].rearrange("(p t) q -> p t q", t=PACK)
-        q_first = keep.tile([P, PACK * P], F32, name="q_first", align_bytes=64)
+        q_first = keep.tile([P, PACK * P], F32, name="q_first", tag="q_first", align_bytes=64)
         nc.sync.dma_start(out=q_first[:].rearrange("p (t q) -> p t q", t=PACK), in_=q_rows[:, :, 0:P])
         q_rest = keep.tile([P, PACK * NQ], F32, name="q_rest", align_bytes=64)
         rest_rows = q_rest[:].rearrange("p (t q) -> p t q", t=PACK)
@@ -48,16 +48,9 @@ def tile_attend_sddmm_kb_kernel(tc, qT, kT, kb, offs, out):
 
         ident = keep.tile([P, P], F32, name="ident")
         make_identity(nc, ident[:])
-        windows = []
-        for m in range(3):
-            window = keep.tile([P, T], F32, name=f"window{m}")
-            windows.append(window)
-        nc.vector.memset(windows[1][:, 0 : T // 2], 0.0)
-        nc.vector.memset(windows[2][:], 0.0)
-        nc.gpsimd.memset(windows[0][:, 0:P], 0.0)
-        nc.gpsimd.memset(windows[0][:, P : 2 * P], 0.0)
-        nc.gpsimd.memset(windows[0][:, 2 * P : T], 0.0)
-        nc.gpsimd.memset(windows[1][:, T // 2 : T], 0.0)
+        windows = [keep.tile([P, T], F32, name=f"window{m}") for m in range(2)]
+        for window in windows:
+            nc.vector.memset(window[:], 0.0)
 
         kb_pool = keep.tile([P, T], F32, name="kb_pool")
         kb_view = kb_pool[:].rearrange("q (p c) -> q p c", c=T // P)
@@ -147,6 +140,8 @@ def tile_attend_sddmm_kb_kernel(tc, qT, kT, kb, offs, out):
         nc.scalar.copy(out=second_raw, in_=acc[:])
         scatter(0, H, H, second_raw)
         nc.sync.dma_start(out=out[0, 0:P, :], in_=windows[0][:])
+        windows.append(keep.tile([P, T], F32, name="window2", tag="q_first", align_bytes=64))
+        nc.gpsimd.memset(windows[2][:], 0.0)
         for m in (1, 2):
             raw = keep.tile([P, N], F32, name=f"raw{m}")
             scores(m, 0, N, f"acc{m + 1}", raw[:])

@@ -116,10 +116,11 @@ def tile_attend_sddmm_kb_kernel(tc, qT, kT, kb, offs, out):
             nc.scalar.copy(out=raw, in_=multiply(m, start, width, tag)[:])
             scatter(m, start, width, raw)
 
-        for t in range(PACK - 1):
+        gather(0, 0, 1)
+        gather(0, 1, 2)
+        nc.vector.tensor_copy(kb_listed, kb_pool[:].indirect(offsets[:]))
+        for t in (1, 2):
             gather(t, 0, 2)
-            if t == 0:
-                nc.vector.tensor_copy(kb_listed, kb_pool[:].indirect(offsets[:]))
         gather(3, 0, 1)
         quantize(runs[:, 0], "first", 0, P)
         quantize(runs[:, 3], "first", P, P)

@@ -49,8 +49,9 @@ def tile_attend_sddmm_kb_kernel(tc, qT, kT, kb, offs, out):
         ident = keep.tile([P, P], F32, name="ident")
         make_identity(nc, ident[:])
         windows = [keep.tile([P, T], F32, name=f"window{m}") for m in range(2)]
-        for window in windows:
-            nc.vector.memset(window[:], 0.0)
+        for cols in (slice(0, T // 2 + 1), slice(T // 2 + 1, T)):
+            nc.vector.memset(windows[0][:, cols], 0.0)
+        nc.vector.memset(windows[1][:], 0.0)
 
         kb_pool = keep.tile([P, T], F32, name="kb_pool")
         kb_view = kb_pool[:].rearrange("q (p c) -> q p c", c=T // P)

@@ -67,8 +67,8 @@ def tile_attend_sddmm_kb_kernel(tc, qT, kT, kb, offs, out):
         kb_listed = stage[:, P * PACK : 3 * P * PACK].bitcast(F32)
         widths = {"first": H, "second": H, 0: P, 1: P, 2: P}
         codes = {k: keep.tile([P, w], U32, name=f"codes_{k}", align_bytes=64) for k, w in widths.items()}
-        scales = {k: keep.tile([P, w], U8, name=f"scales_{k}", align_bytes=64)[:] for k, w in widths.items() if k != 2}
-        scales[2] = scales[0][4:P, :]
+        scales = {k: keep.tile([P, w], U8, name=f"scales_{k}", align_bytes=64)[:] for k, w in widths.items() if k != "second"}
+        scales["second"] = scales["first"][4:P, :]
 
         by_half = stage[:].rearrange("p (h r n t) -> p h r n t", h=2, n=P, t=PACK)[:, :, 0:4:3, :, :]
 
@@ -96,14 +96,16 @@ def tile_attend_sddmm_kb_kernel(tc, qT, kT, kb, offs, out):
 
         def multiply(m, start, width, tag):
             acc = psum.tile([P, width], F32, name=f"acc{m}_{start}", tag=tag)
-            for col in range(0, width, H):
+            step = min(width, H)
+            for col in range(0, width, step):
                 half = "first" if start + col < H else "second"
+                cols = slice((start + col) % H, (start + col) % H + step)
                 nc.tensor.matmul_mx(
-                    out=acc[:, col : col + H],
+                    out=acc[:, col : col + step],
                     lhsT=codes[m][:].bitcast(FP8X4),
                     lhsT_scale=scales[m],
-                    rhs=codes[half][:].bitcast(FP8X4),
-                    rhs_scale=scales[half],
+                    rhs=codes[half][:, cols].bitcast(FP8X4),
+                    rhs_scale=scales[half][:, cols],
                     start=True,
                     stop=True,
                 )
@@ -115,7 +117,6 @@ def tile_attend_sddmm_kb_kernel(tc, qT, kT, kb, offs, out):
 
         def scores(m, start, width, tag, raw):
             nc.scalar.copy(out=raw, in_=multiply(m, start, width, tag)[:])
-            scatter(m, start, width, raw)
 
         gather(0, 0, 1)
         gather(0, 1, 2)
@@ -129,22 +130,26 @@ def tile_attend_sddmm_kb_kernel(tc, qT, kT, kb, offs, out):
         gather(3, 1, 2)
         q_staged = q_first[:, 0:H].bitcast(BF16).rearrange("p (q t) -> p q t", t=PACK)
         queries(1, q_staged)
-        acc = multiply(0, 0, H, "acc0")
         first_raw = q_rest[:, NQ : NQ + H]
-        nc.scalar.copy(out=first_raw, in_=acc[:])
+        scores(0, 0, P, "acc0", first_raw[:, 0:P])
+        scores(0, P, P, "acc1", first_raw[:, P:H])
+        scatter(0, 0, H, first_raw)
+        raw1 = keep.tile([P, N], F32, name="raw1")
+        scores(1, 0, H, "acc2", raw1[:, 0:H])
         quantize(runs[:, 4], "second", 0, P)
         quantize(runs[:, 7], "second", P, P)
-        scatter(0, 0, H, first_raw)
-        lay_out(2, q_staged)
-        acc = multiply(0, H, H, "acc1")
-        quantize(q_staged, 2, 0, P)
+        queries(2, q_staged)
+        scatter(1, 0, H, raw1[:, 0:H])
         second_raw = q_rest[:, 3 * NQ - P : 3 * NQ + P]
-        nc.scalar.copy(out=second_raw, in_=acc[:])
+        scores(0, H, H, "acc3", second_raw)
         scatter(0, H, H, second_raw)
         nc.sync.dma_start(out=out[0, 0:P, :], in_=windows[0][:])
+        scores(1, H, H, "bank0", raw1[:, H:N])
+        scatter(1, H, H, raw1[:, H:N])
+        nc.sync.dma_start(out=out[0, P : 2 * P, :], in_=windows[1][:])
         windows.append(keep.tile([P, T], F32, name="window2", tag="q_first", align_bytes=64))
         nc.gpsimd.memset(windows[2][:], 0.0)
-        for m in (1, 2):
-            raw = keep.tile([P, N], F32, name=f"raw{m}")
-            scores(m, 0, N, f"acc{m + 1}", raw[:])
-            nc.sync.dma_start(out=out[0, m * P : (m + 1) * P, :], in_=windows[m][:])
+        raw2 = keep.tile([P, N], F32, name="raw2")
+        scores(2, 0, N, "bank1", raw2[:])
+        scatter(2, 0, N, raw2[:])
+        nc.sync.dma_start(out=out[0, 2 * P : 3 * P, :], in_=windows[2][:])

@@ -62,19 +62,26 @@ def tile_attend_sddmm_kb_kernel(tc, qT, kT, kb, offs, out):
                 nc.tensor.transpose(bank[:, j, :], kb_part[:, c : c + 1].to_broadcast([P, P]), ident[:])
             nc.scalar.copy(out=kb_view[:, :, 4 * b : 4 * b + 4], in_=bank[:].rearrange("q c p -> q p c"))
 
-        stage = keep.tile([P, 8 * P * PACK], BF16, name="stage", align_bytes=64)
-        runs = stage[:].rearrange("p (r n t) -> p r n t", n=P, t=PACK)
-        kb_listed = stage[:, P * PACK : 3 * P * PACK].bitcast(F32)
+        U = 2 * P
+        stage_a = keep.tile([P, 6 * U], BF16, name="stage_a", align_bytes=64)
+        stage_b = keep.tile([P, 8 * U], BF16, name="stage_b", align_bytes=64)
+        first = stage_a[:].rearrange("p (r n t) -> p r n t", r=3, t=PACK)[:, 0:3:2]
+        kb_first = stage_a[:, 2 * U : 4 * U].bitcast(F32)
+        pairs = stage_b[:].rearrange("p (r j u b a t) -> p r j u a b t", r=4, j=32, u=2, b=2, t=2)[:, 0:4:3]
+        words = stage_b[:].bitcast(U32).rearrange("p (r j u b a) -> p r j a b u", r=4, j=32, u=2, b=2)[:, 0:4:3]
+        q0_tile = keep.tile([P, 2 * U], BF16, name="q0_staged", align_bytes=64)
+        q0_staged = q0_tile[:].rearrange("p (n t) -> p n t", t=PACK)
+        kb_listed = stage_b[:, 2 * U : 6 * U].bitcast(F32)
+        second = keep.tile([P, H * PACK], BF16, name="second", align_bytes=64)
+        second_runs = second[:].rearrange("p (r n t) -> p r n t", r=2, t=PACK)
+        second_words = second[:].bitcast(U32).rearrange("p (r j a b u) -> p r j a b u", r=2, j=32, a=2, u=2)
         widths = {"first": H, "second": H, 0: P, 1: P, 2: P}
         codes = {k: keep.tile([P, w], U32, name=f"codes_{k}", align_bytes=64) for k, w in widths.items()}
-        scales = {k: keep.tile([P, w], U8, name=f"scales_{k}", align_bytes=64)[:] for k, w in widths.items() if k != "second"}
-        scales["second"] = scales["first"][4:P, :]
+        scales = {k: keep.tile([P, w], U8, name=f"scales_{k}", align_bytes=64)[:] for k, w in widths.items()}
 
-        by_half = stage[:].rearrange("p (h r n t) -> p h r n t", h=2, n=P, t=PACK)[:, :, 0:4:3, :, :]
-
-        def gather(t, first, last):
-            listed = offsets[:, first * H // 16 : last * H // 16]
-            nc.vector.tensor_copy(by_half[:, first:last, :, :, t], planes[t][:].indirect(listed))
+        def gather(t):
+            nc.vector.tensor_copy(first[:, :, :, t], planes[t][:].indirect(offsets[:, 0 : H // 16]))
+            nc.vector.tensor_copy(pairs[:, :, :, t // 2, :, :, t % 2], planes[t][:].indirect(offsets[:, H // 16 : N // 16]))
 
         def quantize(source, key, start, width):
             cols = slice(start, start + width)
@@ -94,14 +101,14 @@ def tile_attend_sddmm_kb_kernel(tc, qT, kT, kb, offs, out):
             lay_out(m, target)
             quantize(target, m, 0, P)
 
-        def multiply(m, start, width, tag):
-            acc = psum.tile([P, width], F32, name=f"acc{m}_{start}", tag=tag)
-            step = min(width, H)
-            for col in range(0, width, step):
-                half = "first" if start + col < H else "second"
-                cols = slice((start + col) % H, (start + col) % H + step)
+        def scores(m, pieces, tag, raw):
+            start = pieces[0][0]
+            acc = psum.tile([P, pieces[-1][1] - start], F32, name=f"acc{m}_{start}", tag=tag)
+            for lo, hi in pieces:
+                half = "first" if lo < H else "second"
+                cols = slice(lo % H, lo % H + hi - lo)
                 nc.tensor.matmul_mx(
-                    out=acc[:, col : col + step],
+                    out=acc[:, lo - start : hi - start],
                     lhsT=codes[m][:].bitcast(FP8X4),
                     lhsT_scale=scales[m],
                     rhs=codes[half][:, cols].bitcast(FP8X4),
@@ -109,47 +116,43 @@ def tile_attend_sddmm_kb_kernel(tc, qT, kT, kb, offs, out):
                     start=True,
                     stop=True,
                 )
-            return acc
+            nc.scalar.copy(out=raw, in_=acc[:])
 
-        def scatter(m, start, width, raw):
-            listed = offsets[:, start // 16 : (start + width) // 16]
-            nc.vector.tensor_tensor(windows[m][:].indirect(listed), raw, kb_listed[:, start : start + width], add)
+        def scatter(m, lo, hi, raw, bias):
+            listed = offsets[:, lo // 16 : hi // 16]
+            nc.vector.tensor_tensor(windows[m][:].indirect(listed), raw, bias[:, lo:hi], add)
 
-        def scores(m, start, width, tag, raw):
-            nc.scalar.copy(out=raw, in_=multiply(m, start, width, tag)[:])
-
-        gather(0, 0, 1)
-        gather(0, 1, 2)
-        nc.vector.tensor_copy(kb_listed, kb_pool[:].indirect(offsets[:]))
-        for t in (1, 2):
-            gather(t, 0, 2)
-        gather(3, 0, 1)
-        quantize(runs[:, 0], "first", 0, P)
-        quantize(runs[:, 3], "first", P, P)
-        queries(0, runs[:, 5])
-        gather(3, 1, 2)
+        gather(0)
+        nc.vector.tensor_copy(kb_first, kb_pool[:].indirect(offsets[:, 0 : H // 16]))
+        nc.vector.tensor_copy(kb_listed[:, H:N], kb_pool[:].indirect(offsets[:, H // 16 : N // 16]))
+        for t in (1, 2, 3):
+            gather(t)
+        queries(0, q0_staged)
+        quantize(first[:, 0], "first", 0, P)
+        quantize(first[:, 1], "first", P, P)
         q_staged = q_first[:, 0:H].bitcast(BF16).rearrange("p (q t) -> p q t", t=PACK)
         queries(1, q_staged)
-        first_raw = q_rest[:, NQ : NQ + H]
-        scores(0, 0, P, "acc0", first_raw[:, 0:P])
-        scores(0, P, P, "acc1", first_raw[:, P:H])
-        scatter(0, 0, H, first_raw)
-        raw1 = keep.tile([P, N], F32, name="raw1")
-        scores(1, 0, H, "acc2", raw1[:, 0:H])
-        quantize(runs[:, 4], "second", 0, P)
-        quantize(runs[:, 7], "second", P, P)
+        for r in range(2):
+            nc.scalar.copy(out=second_words[:, r], in_=words[:, r])
+            quantize(second_runs[:, r], "second", r * P, P)
+        scores(0, [(0, P)], "acc0", kb_listed[:, 0:P])
+        scatter(0, 0, P, kb_listed[:, 0:P], kb_first)
+        raw1a = q_rest[:, NQ : NQ + H]
+        scores(1, [(0, H)], "acc1", raw1a)
+        scatter(1, 0, H, raw1a, kb_first)
         queries(2, q_staged)
-        scatter(1, 0, H, raw1[:, 0:H])
-        second_raw = q_rest[:, 3 * NQ - P : 3 * NQ + P]
-        scores(0, H, H, "acc3", second_raw)
-        scatter(0, H, H, second_raw)
+        nc.scalar.copy(out=kb_listed[:, 0:H], in_=kb_first)
+        raw0 = keep.tile([P, N - P], F32, name="raw0")
+        scores(0, [(P, H), (H, N)], "acc2", raw0[:])
+        scatter(0, P, N, raw0[:], kb_listed)
         nc.sync.dma_start(out=out[0, 0:P, :], in_=windows[0][:])
-        scores(1, H, H, "bank0", raw1[:, H:N])
-        scatter(1, H, H, raw1[:, H:N])
+        raw1b = keep.tile([P, H], F32, name="raw1b")
+        scores(1, [(H, N)], "acc3", raw1b[:])
+        scatter(1, H, N, raw1b[:], kb_listed)
         nc.sync.dma_start(out=out[0, P : 2 * P, :], in_=windows[1][:])
         windows.append(keep.tile([P, T], F32, name="window2", tag="q_first", align_bytes=64))
         nc.gpsimd.memset(windows[2][:], 0.0)
         raw2 = keep.tile([P, N], F32, name="raw2")
-        scores(2, 0, N, "bank1", raw2[:])
-        scatter(2, 0, N, raw2[:])
+        scores(2, [(0, H), (H, N)], "bank0", raw2[:])
+        scatter(2, 0, N, raw2[:], kb_listed)
         nc.sync.dma_start(out=out[0, 2 * P : 3 * P, :], in_=windows[2][:])

@@ -5,6 +5,7 @@ D, T, N, NQ = 512, 2048, 512, 384
 P = 128
 PACK = 4
 H = N // 2
+SHARE = 80
 
 F32 = mybir.dt.float32
 BF16 = mybir.dt.bfloat16
@@ -127,7 +128,14 @@ def tile_attend_sddmm_kb_kernel(tc, qT, kT, kb, offs, out):
         nc.vector.tensor_copy(kb_listed[:, H:N], kb_pool[:].indirect(offsets[:, H // 16 : N // 16]))
         for t in (1, 2, 3):
             gather(t)
-        queries(0, q0_staged)
+        nc.scalar.copy(
+            out=q0_staged[:, 0:SHARE].rearrange("p (c i) t -> p c t i", i=4),
+            in_=q_raw[0][:, :, 0:SHARE].rearrange("p t (c i) -> p c t i", i=4),
+        )
+        nc.gpsimd.tensor_scalar(
+            q0_staged[:, SHARE:P], q_raw[0][:, :, SHARE:P].rearrange("p t q -> p q t"), 1.0, 0.0, mybir.AluOpType.mult, add
+        )
+        quantize(q0_staged, 0, 0, P)
         quantize(first[:, 0], "first", 0, P)
         quantize(first[:, 1], "first", P, P)
         q_staged = q_first[:, 0:H].bitcast(BF16).rearrange("p (q t) -> p q t", t=PACK)

@@ -10,6 +10,7 @@ SHARE = 80
 F32 = mybir.dt.float32
 BF16 = mybir.dt.bfloat16
 U32 = mybir.dt.uint32
+I32 = mybir.dt.int32
 U16 = mybir.dt.uint16
 U8 = mybir.dt.uint8
 FP8X4 = mybir.dt.float8_e4m3fn_x4
@@ -40,7 +41,7 @@ def tile_attend_sddmm_kb_kernel(tc, qT, kT, kb, offs, out):
         q_rows = qT[0].rearrange("(p t) q -> p t q", t=PACK)
         q_first = keep.tile([P, PACK * P], F32, name="q_first", tag="q_first", align_bytes=64)
         nc.sync.dma_start(out=q_first[:].rearrange("p (t q) -> p t q", t=PACK), in_=q_rows[:, :, 0:P])
-        q_rest = keep.tile([P, PACK * NQ], F32, name="q_rest", align_bytes=64)
+        q_rest = keep.tile([P, PACK * NQ], F32, name="q_rest", tag="q_rest", align_bytes=64)
         rest_rows = q_rest[:].rearrange("p (t q) -> p t q", t=PACK)
         q_raw = [q_first[:].rearrange("p (t q) -> p t q", t=PACK)]
         for m in (1, 2):
@@ -65,17 +66,17 @@ def tile_attend_sddmm_kb_kernel(tc, qT, kT, kb, offs, out):
 
         U = 2 * P
         stage_a = keep.tile([P, 6 * U], BF16, name="stage_a", align_bytes=64)
-        stage_b = keep.tile([P, 8 * U], BF16, name="stage_b", align_bytes=64)
+        stage_b = keep.tile([P, 6 * U], BF16, name="stage_b", align_bytes=64)
         first = stage_a[:].rearrange("p (r n t) -> p r n t", r=3, t=PACK)[:, 0:3:2]
         kb_first = stage_a[:, 2 * U : 4 * U].bitcast(F32)
-        pairs = stage_b[:].rearrange("p (r j u b a t) -> p r j u a b t", r=4, j=32, u=2, b=2, t=2)[:, 0:4:3]
-        words = stage_b[:].bitcast(U32).rearrange("p (r j u b a) -> p r j a b u", r=4, j=32, u=2, b=2)[:, 0:4:3]
+        pairs = stage_b[:].rearrange("p (r j u b a t) -> p r j u a b t", r=3, j=32, u=2, b=2, t=2)[:, 0:3:2]
+        words = stage_b[:].bitcast(I32).rearrange("p (r j u b a) -> p r j a b u", r=3, j=32, u=2, b=2)[:, 0:3:2]
         q0_tile = keep.tile([P, 2 * U], BF16, name="q0_staged", align_bytes=64)
         q0_staged = q0_tile[:].rearrange("p (n t) -> p n t", t=PACK)
-        kb_listed = stage_b[:, 2 * U : 6 * U].bitcast(F32)
+        kb_second = stage_b[:, 2 * U : 4 * U].bitcast(F32)
+        kb_listed = stage_a[:, 2 * U : 6 * U].bitcast(F32)
         second = keep.tile([P, H * PACK], BF16, name="second", align_bytes=64)
-        second_runs = second[:].rearrange("p (r n t) -> p r n t", r=2, t=PACK)
-        second_words = second[:].bitcast(U32).rearrange("p (r j a b u) -> p r j a b u", r=2, j=32, a=2, u=2)
+        second_words = second[:].bitcast(I32).rearrange("p (r j a b u) -> p r j a b u", r=2, j=32, a=2, u=2)
         widths = {"first": H, "second": H, 0: P, 1: P, 2: P}
         codes = {k: keep.tile([P, w], U32, name=f"codes_{k}", align_bytes=64) for k, w in widths.items()}
         scales = {k: keep.tile([P, w], U8, name=f"scales_{k}", align_bytes=64)[:] for k, w in widths.items()}
@@ -125,7 +126,7 @@ def tile_attend_sddmm_kb_kernel(tc, qT, kT, kb, offs, out):
 
         gather(0)
         nc.vector.tensor_copy(kb_first, kb_pool[:].indirect(offsets[:, 0 : H // 16]))
-        nc.vector.tensor_copy(kb_listed[:, H:N], kb_pool[:].indirect(offsets[:, H // 16 : N // 16]))
+        nc.vector.tensor_copy(kb_second, kb_pool[:].indirect(offsets[:, H // 16 : N // 16]))
         for t in (1, 2, 3):
             gather(t)
         nc.scalar.copy(
@@ -137,28 +138,31 @@ def tile_attend_sddmm_kb_kernel(tc, qT, kT, kb, offs, out):
         )
         quantize(q0_staged, 0, 0, P)
         quantize(first[:, 0], "first", 0, P)
+        for r in range(2):
+            nc.vector.tensor_copy(second_words[:, r], words[:, r])
         quantize(first[:, 1], "first", P, P)
         q_staged = q_first[:, 0:H].bitcast(BF16).rearrange("p (q t) -> p q t", t=PACK)
+        second_runs = second[:].rearrange("p (r n t) -> p r n t", r=2, t=PACK)
+        quantize(second_runs[:, 0], "second", 0, P)
         queries(1, q_staged)
-        for r in range(2):
-            nc.scalar.copy(out=second_words[:, r], in_=words[:, r])
-            quantize(second_runs[:, r], "second", r * P, P)
-        scores(0, [(0, P)], "acc0", kb_listed[:, 0:P])
-        scatter(0, 0, P, kb_listed[:, 0:P], kb_first)
-        raw1a = q_rest[:, NQ : NQ + H]
-        scores(1, [(0, H)], "acc1", raw1a)
-        scatter(1, 0, H, raw1a, kb_first)
-        queries(2, q_staged)
-        nc.scalar.copy(out=kb_listed[:, 0:H], in_=kb_first)
+        quantize(second_runs[:, 1], "second", P, P)
+        raw0a = keep.tile([P, P], F32, name="raw0a")
+        scores(0, [(0, P)], "acc0", raw0a[:])
+        nc.scalar.copy(out=kb_listed[:, H:N], in_=kb_second)
+        scatter(0, 0, P, raw0a[:], kb_first)
+        raw1a = q_rest[:, NQ : NQ + P]
+        scores(1, [(0, P)], "acc1", raw1a)
+        scatter(1, 0, P, raw1a, kb_first)
+        queries(2, second_runs[:, 0])
         raw0 = keep.tile([P, N - P], F32, name="raw0")
         scores(0, [(P, H), (H, N)], "acc2", raw0[:])
         scatter(0, P, N, raw0[:], kb_listed)
         nc.sync.dma_start(out=out[0, 0:P, :], in_=windows[0][:])
-        raw1b = keep.tile([P, H], F32, name="raw1b")
-        scores(1, [(H, N)], "acc3", raw1b[:])
-        scatter(1, H, N, raw1b[:], kb_listed)
+        raw1b = keep.tile([P, N - P], F32, name="raw1b")
+        scores(1, [(P, H), (H, N)], "acc3", raw1b[:])
+        scatter(1, P, N, raw1b[:], kb_listed)
         nc.sync.dma_start(out=out[0, P : 2 * P, :], in_=windows[1][:])
-        windows.append(keep.tile([P, T], F32, name="window2", tag="q_first", align_bytes=64))
+        windows.append(keep.tile([P, T], F32, name="window2", tag="q_rest", align_bytes=64))
         nc.gpsimd.memset(windows[2][:], 0.0)
         raw2 = keep.tile([P, N], F32, name="raw2")
         scores(2, [(0, H), (H, N)], "bank0", raw2[:])

@@ -5,12 +5,10 @@ D, T, N, NQ = 512, 2048, 512, 384
 P = 128
 PACK = 4
 H = N // 2
-SHARE = 80
 
 F32 = mybir.dt.float32
 BF16 = mybir.dt.bfloat16
 U32 = mybir.dt.uint32
-I32 = mybir.dt.int32
 U16 = mybir.dt.uint16
 U8 = mybir.dt.uint8
 FP8X4 = mybir.dt.float8_e4m3fn_x4
@@ -22,13 +20,14 @@ BYTES = 4 * (D * NQ + D * T + T + NQ * T) + 2 * P * (N // 16)
 def tile_attend_sddmm_kb_kernel(tc, qT, kT, kb, offs, out):
     nc = tc.nc
     add = mybir.AluOpType.add
+    copy = mybir.ActivationFunctionType.Copy
     with (
         tc.tile_pool(name="keep", bufs=1) as keep,
         tc.psum_pool(name="psum", bufs=1) as psum,
     ):
         kb_part = keep.tile([P, T // P], F32, name="kb_part")
-        nc.sync.dma_start(out=kb_part[:], in_=kb[0].rearrange("(p c) -> p c", c=T // P))
         offsets = keep.tile([P, N // 16], U16, name="offsets")
+        listed = [offsets[:, 0 : H // 16], offsets[:, H // 16 : N // 16]]
 
         k_rows = kT.rearrange("(p t) n -> p t n", t=PACK)
         planes = []
@@ -38,24 +37,20 @@ def tile_attend_sddmm_kb_kernel(tc, qT, kT, kb, offs, out):
             planes.append(plane)
             if t == 0:
                 nc.sync.dma_start(offsets[:], offs)
+                nc.sync.dma_start(out=kb_part[:], in_=kb[0].rearrange("(p c) -> p c", c=T // P))
         q_rows = qT[0].rearrange("(p t) q -> p t q", t=PACK)
-        q_first = keep.tile([P, PACK * P], F32, name="q_first", tag="q_first", align_bytes=64)
-        nc.sync.dma_start(out=q_first[:].rearrange("p (t q) -> p t q", t=PACK), in_=q_rows[:, :, 0:P])
-        q_rest = keep.tile([P, PACK * NQ], F32, name="q_rest", tag="q_rest", align_bytes=64)
-        rest_rows = q_rest[:].rearrange("p (t q) -> p t q", t=PACK)
-        q_raw = [q_first[:].rearrange("p (t q) -> p t q", t=PACK)]
-        for m in (1, 2):
-            q_raw.append(rest_rows[:, :, m * P : (m + 1) * P])
-            nc.sync.dma_start(out=q_raw[m], in_=q_rows[:, :, m * P : (m + 1) * P])
+        q_raw = []
+        for m in range(3):
+            raw = keep.tile([P, PACK, P], F32, name=f"q_raw{m}", tag=f"q_raw{m}", align_bytes=64)
+            nc.sync.dma_start(out=raw[:], in_=q_rows[:, :, m * P : (m + 1) * P])
+            q_raw.append(raw)
 
         ident = keep.tile([P, P], F32, name="ident")
         make_identity(nc, ident[:])
-        windows = [keep.tile([P, T], F32, name=f"window{m}") for m in range(2)]
-        for cols in (slice(0, T // 2 + 1), slice(T // 2 + 1, T)):
-            nc.vector.memset(windows[0][:, cols], 0.0)
-        nc.vector.memset(windows[1][:], 0.0)
+        windows = [keep.tile([P, T], F32, name=f"window{m}") for m in range(3)]
+        nc.vector.memset(windows[0][:], 0.0)
 
-        kb_pool = keep.tile([P, T], F32, name="kb_pool")
+        kb_pool = keep.tile([P, T], F32, name="kb_pool", tag="kb_pool", align_bytes=64)
         kb_view = kb_pool[:].rearrange("q (p c) -> q p c", c=T // P)
         for b in range(4):
             bank = psum.tile([P, 4, P], F32, name=f"bank{b}", tag=f"bank{b}")
@@ -64,107 +59,90 @@ def tile_attend_sddmm_kb_kernel(tc, qT, kT, kb, offs, out):
                 nc.tensor.transpose(bank[:, j, :], kb_part[:, c : c + 1].to_broadcast([P, P]), ident[:])
             nc.scalar.copy(out=kb_view[:, :, 4 * b : 4 * b + 4], in_=bank[:].rearrange("q c p -> q p c"))
 
-        U = 2 * P
-        stage_a = keep.tile([P, 6 * U], BF16, name="stage_a", align_bytes=64)
-        stage_b = keep.tile([P, 6 * U], BF16, name="stage_b", align_bytes=64)
-        first = stage_a[:].rearrange("p (r n t) -> p r n t", r=3, t=PACK)[:, 0:3:2]
-        kb_first = stage_a[:, 2 * U : 4 * U].bitcast(F32)
-        pairs = stage_b[:].rearrange("p (r j u b a t) -> p r j u a b t", r=3, j=32, u=2, b=2, t=2)[:, 0:3:2]
-        words = stage_b[:].bitcast(I32).rearrange("p (r j u b a) -> p r j a b u", r=3, j=32, u=2, b=2)[:, 0:3:2]
-        q0_tile = keep.tile([P, 2 * U], BF16, name="q0_staged", align_bytes=64)
-        q0_staged = q0_tile[:].rearrange("p (n t) -> p n t", t=PACK)
-        kb_second = stage_b[:, 2 * U : 4 * U].bitcast(F32)
-        kb_listed = stage_a[:, 2 * U : 6 * U].bitcast(F32)
-        second = keep.tile([P, H * PACK], BF16, name="second", align_bytes=64)
-        second_words = second[:].bitcast(I32).rearrange("p (r j a b u) -> p r j a b u", r=2, j=32, a=2, u=2)
-        widths = {"first": H, "second": H, 0: P, 1: P, 2: P}
-        codes = {k: keep.tile([P, w], U32, name=f"codes_{k}", align_bytes=64) for k, w in widths.items()}
-        scales = {k: keep.tile([P, w], U8, name=f"scales_{k}", align_bytes=64)[:] for k, w in widths.items()}
+        first = keep.tile([P, H, PACK], BF16, name="first", align_bytes=64)
+        second = keep.tile([P, H, PACK], BF16, name="second", align_bytes=64)
+        kb_listed = keep.tile([P, N], F32, name="kb_listed")
+        nc.scalar.activation(kb_listed[:], kb_pool[:].indirect(offsets[:]), copy)
+        kb_first = keep.tile([P, H], F32, name="kb_first", tag="kb_first", align_bytes=64)
+        nc.vector.tensor_copy(kb_first[:], kb_listed[:, 0:H])
+        second_rows = keep.tile([P, 2, H], BF16, name="second_rows", tag="kb_pool", align_bytes=64)
+        codes, scales = {}, {}
 
-        def gather(t):
-            nc.vector.tensor_copy(first[:, :, :, t], planes[t][:].indirect(offsets[:, 0 : H // 16]))
-            nc.vector.tensor_copy(pairs[:, :, :, t // 2, :, :, t % 2], planes[t][:].indirect(offsets[:, H // 16 : N // 16]))
-
-        def quantize(source, key, start, width):
-            cols = slice(start, start + width)
+        def quantize(source, key, tag):
+            width = source.shape[1]
+            codes[key] = keep.tile([P, width], U32, name=f"codes_{key}", tag=tag, align_bytes=64)
+            scales[key] = keep.tile([P, width], U8, name=f"scales_{key}", align_bytes=64)
             nc.vector.quantize_mx(
-                out=codes[key][:, cols].bitcast(FP8X4),
-                scales=scales[key][:, cols],
-                in_=source.rearrange("p n t -> p (n t)"),
+                out=codes[key][:].bitcast(FP8X4), scales=scales[key][:], in_=source.rearrange("p n t -> p (n t)")
             )
 
-        def lay_out(m, target):
-            nc.scalar.copy(
-                out=target.rearrange("p (c i) t -> p c t i", i=4),
-                in_=q_raw[m].rearrange("p t (c i) -> p c t i", i=4),
+        def scores(acc, m, half):
+            nc.tensor.matmul_mx(
+                out=acc,
+                lhsT=codes[m][:].bitcast(FP8X4),
+                lhsT_scale=scales[m][:],
+                rhs=codes[half][:].bitcast(FP8X4),
+                rhs_scale=scales[half][:],
+                start=True,
+                stop=True,
             )
 
-        def queries(m, target):
-            lay_out(m, target)
-            quantize(target, m, 0, P)
+        def woven(target):
+            return target.rearrange("p (c i) t -> p c t i", i=4)
 
-        def scores(m, pieces, tag, raw):
-            start = pieces[0][0]
-            acc = psum.tile([P, pieces[-1][1] - start], F32, name=f"acc{m}_{start}", tag=tag)
-            for lo, hi in pieces:
-                half = "first" if lo < H else "second"
-                cols = slice(lo % H, lo % H + hi - lo)
-                nc.tensor.matmul_mx(
-                    out=acc[:, lo - start : hi - start],
-                    lhsT=codes[m][:].bitcast(FP8X4),
-                    lhsT_scale=scales[m],
-                    rhs=codes[half][:, cols].bitcast(FP8X4),
-                    rhs_scale=scales[half][:, cols],
-                    start=True,
-                    stop=True,
-                )
-            nc.scalar.copy(out=raw, in_=acc[:])
+        def rows(source):
+            return source.rearrange("p t (c i) -> p c t i", i=4)
 
-        def scatter(m, lo, hi, raw, bias):
-            listed = offsets[:, lo // 16 : hi // 16]
-            nc.vector.tensor_tensor(windows[m][:].indirect(listed), raw, bias[:, lo:hi], add)
+        for t in range(PACK):
+            nc.vector.tensor_copy(first[:, :, t], planes[t][:].indirect(listed[0]))
+            if t < 2:
+                nc.vector.tensor_copy(second[:, :, t], planes[t][:].indirect(listed[1]))
+            else:
+                nc.scalar.activation(second_rows[:, t - 2, :], planes[t][:].indirect(listed[1]), copy)
+                nc.scalar.copy(out=second[:, :, t], in_=second_rows[:, t - 2, :])
+        for m in (1, 2):
+            nc.vector.memset(windows[m][:], 0.0)
 
-        gather(0)
-        nc.vector.tensor_copy(kb_first, kb_pool[:].indirect(offsets[:, 0 : H // 16]))
-        nc.vector.tensor_copy(kb_second, kb_pool[:].indirect(offsets[:, H // 16 : N // 16]))
-        for t in (1, 2, 3):
-            gather(t)
-        nc.scalar.copy(
-            out=q0_staged[:, 0:SHARE].rearrange("p (c i) t -> p c t i", i=4),
-            in_=q_raw[0][:, :, 0:SHARE].rearrange("p t (c i) -> p c t i", i=4),
-        )
-        nc.gpsimd.tensor_scalar(
-            q0_staged[:, SHARE:P], q_raw[0][:, :, SHARE:P].rearrange("p t q -> p q t"), 1.0, 0.0, mybir.AluOpType.mult, add
-        )
-        quantize(q0_staged, 0, 0, P)
-        quantize(first[:, 0], "first", 0, P)
-        for r in range(2):
-            nc.vector.tensor_copy(second_words[:, r], words[:, r])
-        quantize(first[:, 1], "first", P, P)
-        q_staged = q_first[:, 0:H].bitcast(BF16).rearrange("p (q t) -> p q t", t=PACK)
-        second_runs = second[:].rearrange("p (r n t) -> p r n t", r=2, t=PACK)
-        quantize(second_runs[:, 0], "second", 0, P)
-        queries(1, q_staged)
-        quantize(second_runs[:, 1], "second", P, P)
-        raw0a = keep.tile([P, P], F32, name="raw0a")
-        scores(0, [(0, P)], "acc0", raw0a[:])
-        nc.scalar.copy(out=kb_listed[:, H:N], in_=kb_second)
-        scatter(0, 0, P, raw0a[:], kb_first)
-        raw1a = q_rest[:, NQ : NQ + P]
-        scores(1, [(0, P)], "acc1", raw1a)
-        scatter(1, 0, P, raw1a, kb_first)
-        queries(2, second_runs[:, 0])
-        raw0 = keep.tile([P, N - P], F32, name="raw0")
-        scores(0, [(P, H), (H, N)], "acc2", raw0[:])
-        scatter(0, P, N, raw0[:], kb_listed)
+        q0_staged = keep.tile([P, P, PACK], BF16, name="q0_staged", tag="q0_staged", align_bytes=64)
+        nc.vector.tensor_copy(woven(q0_staged[:]), rows(q_raw[0][:]))
+        quantize(first[:], "first", "q_raw0")
+        quantize(q0_staged[:], 0, "codes_0")
+        quantize(second[:], "second", "q0_staged")
+        biased0 = keep.tile([P, N], F32, name="biased0")
+        acc = psum.tile([P, H], F32, name="acc0a", tag="acc0a")
+        scores(acc[:], 0, "first")
+        nc.vector.tensor_tensor(biased0[:, 0:H], acc[:], kb_first[:], add)
+        nc.scalar.activation(windows[0][:].indirect(listed[0]), biased0[:, 0:H], copy)
+
+        q1_staged = keep.tile([P, P, PACK], BF16, name="q1_staged", align_bytes=64)
+        nc.scalar.copy(out=woven(q1_staged[:]), in_=rows(q_raw[1][:]))
+        quantize(q1_staged[:], 1, "kb_first")
+        acc = psum.tile([P, H], F32, name="acc0b", tag="acc0b")
+        scores(acc[:], 0, "second")
+        nc.vector.tensor_tensor(biased0[:, H:N], acc[:], kb_listed[:, H:N], add)
+        nc.scalar.activation(windows[0][:].indirect(listed[1]), biased0[:, H:N], copy)
         nc.sync.dma_start(out=out[0, 0:P, :], in_=windows[0][:])
-        raw1b = keep.tile([P, N - P], F32, name="raw1b")
-        scores(1, [(P, H), (H, N)], "acc3", raw1b[:])
-        scatter(1, P, N, raw1b[:], kb_listed)
+
+        q2_staged = keep.tile([P, P, PACK], BF16, name="q2_staged", align_bytes=64)
+        nc.vector.tensor_copy(woven(q2_staged[:]), rows(q_raw[2][:]))
+        biased1 = keep.tile([P, H], F32, name="biased1")
+        acc = psum.tile([P, H], F32, name="acc1a", tag="acc1a")
+        scores(acc[:], 1, "first")
+        nc.vector.tensor_tensor(biased1[:], acc[:], kb_listed[:, 0:H], add)
+        quantize(q2_staged[:], 2, "codes_2")
+        nc.vector.tensor_copy(windows[1][:].indirect(listed[0]), biased1[:])
+        biased12 = keep.tile([P, 2, H], F32, name="biased12")
+        acc = psum.tile([P, 2, H], F32, name="acc12b", tag="acc12b")
+        scores(acc[:, 0, :], 1, "second")
+        scores(acc[:, 1, :], 2, "second")
+        nc.vector.tensor_tensor(biased12[:], acc[:], kb_listed[:, H:N].unsqueeze(1).to_broadcast([P, 2, H]), add)
+        nc.vector.tensor_copy(windows[1][:].indirect(listed[1]), biased12[:, 0, :])
         nc.sync.dma_start(out=out[0, P : 2 * P, :], in_=windows[1][:])
-        windows.append(keep.tile([P, T], F32, name="window2", tag="q_rest", align_bytes=64))
-        nc.gpsimd.memset(windows[2][:], 0.0)
-        raw2 = keep.tile([P, N], F32, name="raw2")
-        scores(2, [(0, H), (H, N)], "bank0", raw2[:])
-        scatter(2, 0, N, raw2[:], kb_listed)
+
+        raw2 = keep.tile([P, H], F32, name="raw2")
+        acc = psum.tile([P, H], F32, name="acc2a", tag="bank0")
+        scores(acc[:], 2, "first")
+        nc.scalar.copy(out=raw2[:], in_=acc[:])
+        nc.scalar.activation(windows[2][:].indirect(listed[1]), biased12[:, 1, :], copy)
+        nc.vector.tensor_tensor(windows[2][:].indirect(listed[0]), raw2[:], kb_listed[:, 0:H], add)
         nc.sync.dma_start(out=out[0, 2 * P : 3 * P, :], in_=windows[2][:])

@@ -26,6 +26,7 @@ def tile_attend_sddmm_kb_kernel(tc, qT, kT, kb, offs, out):
         tc.psum_pool(name="psum", bufs=1) as psum,
     ):
         kb_part = keep.tile([P, T // P], F32, name="kb_part")
+        nc.sync.dma_start(out=kb_part[:], in_=kb[0].rearrange("(p c) -> p c", c=T // P))
         offsets = keep.tile([P, N // 16], U16, name="offsets")
         listed = [offsets[:, 0 : H // 16], offsets[:, H // 16 : N // 16]]
 
@@ -37,7 +38,6 @@ def tile_attend_sddmm_kb_kernel(tc, qT, kT, kb, offs, out):
             planes.append(plane)
             if t == 0:
                 nc.sync.dma_start(offsets[:], offs)
-                nc.sync.dma_start(out=kb_part[:], in_=kb[0].rearrange("(p c) -> p c", c=T // P))
         q_rows = qT[0].rearrange("(p t) q -> p t q", t=PACK)
         q_raw = []
         for m in range(3):
@@ -48,7 +48,8 @@ def tile_attend_sddmm_kb_kernel(tc, qT, kT, kb, offs, out):
         ident = keep.tile([P, P], F32, name="ident")
         make_identity(nc, ident[:])
         windows = [keep.tile([P, T], F32, name=f"window{m}") for m in range(3)]
-        nc.vector.memset(windows[0][:], 0.0)
+        for cols in (slice(0, T // 2 + 1), slice(T // 2 + 1, T)):
+            nc.vector.memset(windows[0][:, cols], 0.0)
 
         kb_pool = keep.tile([P, T], F32, name="kb_pool", tag="kb_pool", align_bytes=64)
         kb_view = kb_pool[:].rearrange("q (p c) -> q p c", c=T // P)
@@ -99,7 +100,7 @@ def tile_attend_sddmm_kb_kernel(tc, qT, kT, kb, offs, out):
                 nc.vector.tensor_copy(second[:, :, t], planes[t][:].indirect(listed[1]))
             else:
                 nc.scalar.activation(second_rows[:, t - 2, :], planes[t][:].indirect(listed[1]), copy)
-                nc.scalar.copy(out=second[:, :, t], in_=second_rows[:, t - 2, :])
+        nc.scalar.copy(out=woven(second[:, :, 2:4]), in_=rows(second_rows[:]))
         for m in (1, 2):
             nc.vector.memset(windows[m][:], 0.0)
 

@@ -5,6 +5,7 @@ D, T, N, NQ = 512, 2048, 512, 384
 P = 128
 PACK = 4
 H = N // 2
+SHARE = 80
 
 F32 = mybir.dt.float32
 BF16 = mybir.dt.bfloat16
@@ -23,6 +24,7 @@ def tile_attend_sddmm_kb_kernel(tc, qT, kT, kb, offs, out):
     copy = mybir.ActivationFunctionType.Copy
     with (
         tc.tile_pool(name="keep", bufs=1) as keep,
+        tc.tile_pool(name="shared", bufs=1) as shared,
         tc.psum_pool(name="psum", bufs=1) as psum,
     ):
         kb_part = keep.tile([P, T // P], F32, name="kb_part")
@@ -39,11 +41,10 @@ def tile_attend_sddmm_kb_kernel(tc, qT, kT, kb, offs, out):
             if t == 0:
                 nc.sync.dma_start(offsets[:], offs)
         q_rows = qT[0].rearrange("(p t) q -> p t q", t=PACK)
-        q_raw = []
-        for m in range(3):
-            raw = keep.tile([P, PACK, P], F32, name=f"q_raw{m}", tag=f"q_raw{m}", align_bytes=64)
-            nc.sync.dma_start(out=raw[:], in_=q_rows[:, :, m * P : (m + 1) * P])
-            q_raw.append(raw)
+        q_first = keep.tile([P, PACK, P], F32, name="q_first")
+        nc.sync.dma_start(out=q_first[:], in_=q_rows[:, :, 0:P])
+        q_rest = keep.tile([P, PACK, 2 * P], F32, name="q_rest")
+        nc.sync.dma_start(out=q_rest[:], in_=q_rows[:, :, P:NQ])
 
         ident = keep.tile([P, P], F32, name="ident")
         make_identity(nc, ident[:])
@@ -64,26 +65,32 @@ def tile_attend_sddmm_kb_kernel(tc, qT, kT, kb, offs, out):
         second = keep.tile([P, H, PACK], BF16, name="second", align_bytes=64)
         kb_listed = keep.tile([P, N], F32, name="kb_listed")
         nc.scalar.activation(kb_listed[:], kb_pool[:].indirect(offsets[:]), copy)
-        kb_first = keep.tile([P, H], F32, name="kb_first", tag="kb_first", align_bytes=64)
-        nc.vector.tensor_copy(kb_first[:], kb_listed[:, 0:H])
-        second_rows = keep.tile([P, 2, H], BF16, name="second_rows", tag="kb_pool", align_bytes=64)
+        kb_first = shared.tile([P, P], F32, name="kb_first", align_bytes=64, offset=0)
+        nc.vector.tensor_copy(kb_first[:], kb_listed[:, 0:P])
+        stage = keep.tile([P, 4 * H], BF16, name="stage", tag="kb_pool", align_bytes=64)
+        second_rows = stage[:].rearrange("p (r n) -> p r n", n=H)[:, 0:4:3]
+        q0_staged = stage[:, H : 3 * H].rearrange("p (n t) -> p n t", t=PACK)
         codes, scales = {}, {}
+        scale_offsets = {"second": 0, 1: H, 2: H + P}
 
-        def quantize(source, key, tag):
+        def quantize(source, key):
             width = source.shape[1]
-            codes[key] = keep.tile([P, width], U32, name=f"codes_{key}", tag=tag, align_bytes=64)
-            scales[key] = keep.tile([P, width], U8, name=f"scales_{key}", align_bytes=64)
+            codes[key] = keep.tile([P, width], U32, name=f"codes_{key}", align_bytes=64)
+            if key in scale_offsets:
+                scales[key] = shared.tile([P, width], U8, name=f"scales_{key}", align_bytes=64, offset=scale_offsets[key])
+            else:
+                scales[key] = keep.tile([P, width], U8, name=f"scales_{key}", align_bytes=64)
             nc.vector.quantize_mx(
                 out=codes[key][:].bitcast(FP8X4), scales=scales[key][:], in_=source.rearrange("p n t -> p (n t)")
             )
 
-        def scores(acc, m, half):
+        def scores(acc, m, half, cols=slice(0, H)):
             nc.tensor.matmul_mx(
                 out=acc,
                 lhsT=codes[m][:].bitcast(FP8X4),
                 lhsT_scale=scales[m][:],
-                rhs=codes[half][:].bitcast(FP8X4),
-                rhs_scale=scales[half][:],
+                rhs=codes[half][:, cols].bitcast(FP8X4),
+                rhs_scale=scales[half][:, cols],
                 start=True,
                 stop=True,
             )
@@ -94,56 +101,60 @@ def tile_attend_sddmm_kb_kernel(tc, qT, kT, kb, offs, out):
         def rows(source):
             return source.rearrange("p t (c i) -> p c t i", i=4)
 
+        def stage_on_gpsimd(target, source):
+            nc.gpsimd.tensor_scalar(target, source.rearrange("p t q -> p q t"), 1.0, 0.0, mybir.AluOpType.mult, add)
+
         for t in range(PACK):
             nc.vector.tensor_copy(first[:, :, t], planes[t][:].indirect(listed[0]))
             if t < 2:
                 nc.vector.tensor_copy(second[:, :, t], planes[t][:].indirect(listed[1]))
             else:
                 nc.scalar.activation(second_rows[:, t - 2, :], planes[t][:].indirect(listed[1]), copy)
-        nc.scalar.copy(out=woven(second[:, :, 2:4]), in_=rows(second_rows[:]))
         for m in (1, 2):
             nc.vector.memset(windows[m][:], 0.0)
 
-        q0_staged = keep.tile([P, P, PACK], BF16, name="q0_staged", tag="q0_staged", align_bytes=64)
-        nc.vector.tensor_copy(woven(q0_staged[:]), rows(q_raw[0][:]))
-        quantize(first[:], "first", "q_raw0")
-        quantize(q0_staged[:], 0, "codes_0")
-        quantize(second[:], "second", "q0_staged")
+        nc.scalar.copy(out=woven(q0_staged[:, 0:SHARE]), in_=rows(q_first[:, :, 0:SHARE]))
+        stage_on_gpsimd(q0_staged[:, SHARE:P], q_first[:, :, SHARE:P])
+        nc.scalar.copy(out=woven(second[:, :, 2:4]), in_=rows(second_rows))
+        quantize(first[:], "first")
+        quantize(q0_staged, 0)
+        q1_staged = keep.tile([P, P, PACK], BF16, name="q1_staged", align_bytes=64)
+        stage_on_gpsimd(q1_staged[:], q_rest[:, :, 0:P])
+        q2_staged = keep.tile([P, P, PACK], BF16, name="q2_staged", align_bytes=64)
+        nc.scalar.copy(out=woven(q2_staged[:]), in_=rows(q_rest[:, :, P : 2 * P]))
         biased0 = keep.tile([P, N], F32, name="biased0")
-        acc = psum.tile([P, H], F32, name="acc0a", tag="acc0a")
-        scores(acc[:], 0, "first")
-        nc.vector.tensor_tensor(biased0[:, 0:H], acc[:], kb_first[:], add)
+        for r, bias in enumerate((kb_first[:], kb_listed[:, P:H])):
+            cols = slice(r * P, (r + 1) * P)
+            acc = psum.tile([P, P], F32, name=f"acc0a{r}", tag=f"acc0a{r}")
+            scores(acc[:], 0, "first", cols)
+            nc.vector.tensor_tensor(biased0[:, cols], acc[:], bias, add)
         nc.scalar.activation(windows[0][:].indirect(listed[0]), biased0[:, 0:H], copy)
 
-        q1_staged = keep.tile([P, P, PACK], BF16, name="q1_staged", align_bytes=64)
-        nc.scalar.copy(out=woven(q1_staged[:]), in_=rows(q_raw[1][:]))
-        quantize(q1_staged[:], 1, "kb_first")
+        quantize(second[:], "second")
+        quantize(q1_staged[:], 1)
+        quantize(q2_staged[:], 2)
         acc = psum.tile([P, H], F32, name="acc0b", tag="acc0b")
         scores(acc[:], 0, "second")
         nc.vector.tensor_tensor(biased0[:, H:N], acc[:], kb_listed[:, H:N], add)
         nc.scalar.activation(windows[0][:].indirect(listed[1]), biased0[:, H:N], copy)
         nc.sync.dma_start(out=out[0, 0:P, :], in_=windows[0][:])
 
-        q2_staged = keep.tile([P, P, PACK], BF16, name="q2_staged", align_bytes=64)
-        nc.vector.tensor_copy(woven(q2_staged[:]), rows(q_raw[2][:]))
-        biased1 = keep.tile([P, H], F32, name="biased1")
-        acc = psum.tile([P, H], F32, name="acc1a", tag="acc1a")
-        scores(acc[:], 1, "first")
-        nc.vector.tensor_tensor(biased1[:], acc[:], kb_listed[:, 0:H], add)
-        quantize(q2_staged[:], 2, "codes_2")
-        nc.vector.tensor_copy(windows[1][:].indirect(listed[0]), biased1[:])
-        biased12 = keep.tile([P, 2, H], F32, name="biased12")
-        acc = psum.tile([P, 2, H], F32, name="acc12b", tag="acc12b")
-        scores(acc[:, 0, :], 1, "second")
-        scores(acc[:, 1, :], 2, "second")
-        nc.vector.tensor_tensor(biased12[:], acc[:], kb_listed[:, H:N].unsqueeze(1).to_broadcast([P, 2, H]), add)
-        nc.vector.tensor_copy(windows[1][:].indirect(listed[1]), biased12[:, 0, :])
+        biased1 = keep.tile([P, N], F32, name="biased1")
+        acc = psum.tile([P, N], F32, name="acc1", tag="acc1")
+        scores(acc[:, 0:H], 1, "first")
+        scores(acc[:, H:N], 1, "second")
+        nc.vector.tensor_tensor(biased1[:], acc[:], kb_listed[:], add)
+        biased2 = keep.tile([P, H], F32, name="biased2")
+        acc = psum.tile([P, H], F32, name="acc2b", tag="bank0")
+        scores(acc[:], 2, "second")
+        nc.vector.tensor_tensor(biased2[:], acc[:], kb_listed[:, H:N], add)
+        nc.vector.tensor_copy(windows[1][:].indirect(offsets[:]), biased1[:])
         nc.sync.dma_start(out=out[0, P : 2 * P, :], in_=windows[1][:])
 
         raw2 = keep.tile([P, H], F32, name="raw2")
-        acc = psum.tile([P, H], F32, name="acc2a", tag="bank0")
+        acc = psum.tile([P, H], F32, name="acc2a", tag="bank1")
         scores(acc[:], 2, "first")
         nc.scalar.copy(out=raw2[:], in_=acc[:])
-        nc.scalar.activation(windows[2][:].indirect(listed[1]), biased12[:, 1, :], copy)
+        nc.scalar.activation(windows[2][:].indirect(listed[1]), biased2[:], copy)
         nc.vector.tensor_tensor(windows[2][:].indirect(listed[0]), raw2[:], kb_listed[:, 0:H], add)
         nc.sync.dma_start(out=out[0, 2 * P : 3 * P, :], in_=windows[2][:])

@@ -5,7 +5,7 @@ D, T, N, NQ = 512, 2048, 512, 384
 P = 128
 PACK = 4
 H = N // 2
-SHARE = 80
+SHARE = 64
 
 F32 = mybir.dt.float32
 BF16 = mybir.dt.bfloat16
@@ -41,7 +41,7 @@ def tile_attend_sddmm_kb_kernel(tc, qT, kT, kb, offs, out):
             if t == 0:
                 nc.sync.dma_start(offsets[:], offs)
         q_rows = qT[0].rearrange("(p t) q -> p t q", t=PACK)
-        q_first = keep.tile([P, PACK, P], F32, name="q_first")
+        q_first = keep.tile([P, PACK, P], F32, name="q_first", tag="q_first", align_bytes=64)
         nc.sync.dma_start(out=q_first[:], in_=q_rows[:, :, 0:P])
         q_rest = keep.tile([P, PACK, 2 * P], F32, name="q_rest")
         nc.sync.dma_start(out=q_rest[:], in_=q_rows[:, :, P:NQ])
@@ -75,7 +75,8 @@ def tile_attend_sddmm_kb_kernel(tc, qT, kT, kb, offs, out):
 
         def quantize(source, key):
             width = source.shape[1]
-            codes[key] = keep.tile([P, width], U32, name=f"codes_{key}", align_bytes=64)
+            tag = "q_first" if key == "run1" else f"codes_{key}"
+            codes[key] = keep.tile([P, width], U32, name=f"codes_{key}", tag=tag, align_bytes=64)
             if key in scale_offsets:
                 scales[key] = shared.tile([P, width], U8, name=f"scales_{key}", align_bytes=64, offset=scale_offsets[key])
             else:
@@ -84,13 +85,13 @@ def tile_attend_sddmm_kb_kernel(tc, qT, kT, kb, offs, out):
                 out=codes[key][:].bitcast(FP8X4), scales=scales[key][:], in_=source.rearrange("p n t -> p (n t)")
             )
 
-        def scores(acc, m, half, cols=slice(0, H)):
+        def scores(acc, m, half):
             nc.tensor.matmul_mx(
                 out=acc,
                 lhsT=codes[m][:].bitcast(FP8X4),
                 lhsT_scale=scales[m][:],
-                rhs=codes[half][:, cols].bitcast(FP8X4),
-                rhs_scale=scales[half][:, cols],
+                rhs=codes[half][:].bitcast(FP8X4),
+                rhs_scale=scales[half][:],
                 start=True,
                 stop=True,
             )
@@ -116,8 +117,9 @@ def tile_attend_sddmm_kb_kernel(tc, qT, kT, kb, offs, out):
         nc.scalar.copy(out=woven(q0_staged[:, 0:SHARE]), in_=rows(q_first[:, :, 0:SHARE]))
         stage_on_gpsimd(q0_staged[:, SHARE:P], q_first[:, :, SHARE:P])
         nc.scalar.copy(out=woven(second[:, :, 2:4]), in_=rows(second_rows))
-        quantize(first[:], "first")
+        quantize(first[:, 0:P], "run0")
         quantize(q0_staged, 0)
+        quantize(first[:, P:H], "run1")
         q1_staged = keep.tile([P, P, PACK], BF16, name="q1_staged", align_bytes=64)
         stage_on_gpsimd(q1_staged[:], q_rest[:, :, 0:P])
         q2_staged = keep.tile([P, P, PACK], BF16, name="q2_staged", align_bytes=64)
@@ -126,7 +128,7 @@ def tile_attend_sddmm_kb_kernel(tc, qT, kT, kb, offs, out):
         for r, bias in enumerate((kb_first[:], kb_listed[:, P:H])):
             cols = slice(r * P, (r + 1) * P)
             acc = psum.tile([P, P], F32, name=f"acc0a{r}", tag=f"acc0a{r}")
-            scores(acc[:], 0, "first", cols)
+            scores(acc[:], 0, f"run{r}")
             nc.vector.tensor_tensor(biased0[:, cols], acc[:], bias, add)
         nc.scalar.activation(windows[0][:].indirect(listed[0]), biased0[:, 0:H], copy)
 
@@ -141,7 +143,8 @@ def tile_attend_sddmm_kb_kernel(tc, qT, kT, kb, offs, out):
 
         biased1 = keep.tile([P, N], F32, name="biased1")
         acc = psum.tile([P, N], F32, name="acc1", tag="acc1")
-        scores(acc[:, 0:H], 1, "first")
+        scores(acc[:, 0:P], 1, "run0")
+        scores(acc[:, P:H], 1, "run1")
         scores(acc[:, H:N], 1, "second")
         nc.vector.tensor_tensor(biased1[:], acc[:], kb_listed[:], add)
         biased2 = keep.tile([P, H], F32, name="biased2")
@@ -153,7 +156,8 @@ def tile_attend_sddmm_kb_kernel(tc, qT, kT, kb, offs, out):
 
         raw2 = keep.tile([P, H], F32, name="raw2")
         acc = psum.tile([P, H], F32, name="acc2a", tag="bank1")
-        scores(acc[:], 2, "first")
+        scores(acc[:, 0:P], 2, "run0")
+        scores(acc[:, P:H], 2, "run1")
         nc.scalar.copy(out=raw2[:], in_=acc[:])
         nc.scalar.activation(windows[2][:].indirect(listed[1]), biased2[:], copy)
         nc.vector.tensor_tensor(windows[2][:].indirect(listed[0]), raw2[:], kb_listed[:, 0:H], add)

@@ -66,10 +66,10 @@ def tile_attend_sddmm_kb_kernel(tc, qT, kT, kb, offs, out):
         kb_listed = keep.tile([P, N], F32, name="kb_listed")
         nc.scalar.activation(kb_listed[:], kb_pool[:].indirect(offsets[:]), copy)
         kb_first = shared.tile([P, P], F32, name="kb_first", align_bytes=64, offset=0)
-        nc.vector.tensor_copy(kb_first[:], kb_listed[:, 0:P])
+        nc.scalar.copy(out=kb_first[:], in_=kb_listed[:, 0:P])
         stage = keep.tile([P, 4 * H], BF16, name="stage", tag="kb_pool", align_bytes=64)
-        second_rows = stage[:].rearrange("p (r n) -> p r n", n=H)[:, 0:4:3]
-        q0_staged = stage[:, H : 3 * H].rearrange("p (n t) -> p n t", t=PACK)
+        second_rows = stage[:, 0 : 2 * H].rearrange("p (r n) -> p r n", n=H)
+        q0_staged = stage[:, 2 * H : 4 * H].rearrange("p (n t) -> p n t", t=PACK)
         codes, scales = {}, {}
         scale_offsets = {"second": 0, 1: H, 2: H + P}
 

@@ -35,20 +35,20 @@ def tile_attend_sddmm_kb_kernel(tc, qT, kT, kb, offs, out):
         k_rows = kT.rearrange("(p t) n -> p t n", t=PACK)
         planes = []
         for t in range(PACK):
-            plane = keep.tile([P, T], F32, name=f"plane{t}")
+            plane = keep.tile([P, T], F32, name=f"plane{t}", align_bytes=256)
             nc.sync.dma_start(out=plane[:], in_=k_rows[:, t, :])
             planes.append(plane)
             if t == 0:
                 nc.sync.dma_start(offsets[:], offs)
         q_rows = qT[0].rearrange("(p t) q -> p t q", t=PACK)
-        q_first = keep.tile([P, PACK, P], F32, name="q_first", tag="q_first", align_bytes=64)
+        q_first = keep.tile([P, PACK, P], F32, name="q_first", tag="q_first", align_bytes=256)
         nc.sync.dma_start(out=q_first[:], in_=q_rows[:, :, 0:P])
-        q_rest = keep.tile([P, PACK, 2 * P], F32, name="q_rest")
+        q_rest = keep.tile([P, PACK, 2 * P], F32, name="q_rest", align_bytes=256)
         nc.sync.dma_start(out=q_rest[:], in_=q_rows[:, :, P:NQ])
 
         ident = keep.tile([P, P], F32, name="ident")
         make_identity(nc, ident[:])
-        windows = [keep.tile([P, T], F32, name=f"window{m}") for m in range(3)]
+        windows = [keep.tile([P, T], F32, name=f"window{m}", align_bytes=256) for m in range(3)]
         for cols in (slice(0, T // 2 + 1), slice(T // 2 + 1, T)):
             nc.vector.memset(windows[0][:, cols], 0.0)
 
@@ -76,7 +76,7 @@ def tile_attend_sddmm_kb_kernel(tc, qT, kT, kb, offs, out):
         def quantize(source, key):
             width = source.shape[1]
             tag = "q_first" if key == "run1" else f"codes_{key}"
-            codes[key] = keep.tile([P, width], U32, name=f"codes_{key}", tag=tag, align_bytes=64)
+            codes[key] = keep.tile([P, width], U32, name=f"codes_{key}", tag=tag, align_bytes=256)
             if key in scale_offsets:
                 scales[key] = shared.tile([P, width], U8, name=f"scales_{key}", align_bytes=64, offset=scale_offsets[key])
             else:

@@ -35,7 +35,7 @@ def tile_attend_sddmm_kb_kernel(tc, qT, kT, kb, offs, out):
         k_rows = kT.rearrange("(p t) n -> p t n", t=PACK)
         planes = []
         for t in range(PACK):
-            plane = keep.tile([P, T], F32, name=f"plane{t}", align_bytes=256)
+            plane = keep.tile([P, T], F32, name=f"plane{t}", tag=f"plane{t}", align_bytes=256)
             nc.sync.dma_start(out=plane[:], in_=k_rows[:, t, :])
             planes.append(plane)
             if t == 0:
@@ -75,7 +75,7 @@ def tile_attend_sddmm_kb_kernel(tc, qT, kT, kb, offs, out):
 
         def quantize(source, key):
             width = source.shape[1]
-            tag = "q_first" if key == "run1" else f"codes_{key}"
+            tag = {"run0": "plane3", "run1": "q_first"}.get(key, f"codes_{key}")
             codes[key] = keep.tile([P, width], U32, name=f"codes_{key}", tag=tag, align_bytes=256)
             if key in scale_offsets:
                 scales[key] = shared.tile([P, width], U8, name=f"scales_{key}", align_bytes=64, offset=scale_offsets[key])
@@ -115,15 +115,15 @@ def tile_attend_sddmm_kb_kernel(tc, qT, kT, kb, offs, out):
             nc.vector.memset(windows[m][:], 0.0)
 
         nc.scalar.copy(out=woven(q0_staged[:, 0:SHARE]), in_=rows(q_first[:, :, 0:SHARE]))
-        stage_on_gpsimd(q0_staged[:, SHARE:P], q_first[:, :, SHARE:P])
+        nc.vector.tensor_copy(woven(q0_staged[:, SHARE:P]), rows(q_first[:, :, SHARE:P]))
         nc.scalar.copy(out=woven(second[:, :, 2:4]), in_=rows(second_rows))
         quantize(first[:, 0:P], "run0")
         quantize(q0_staged, 0)
         quantize(first[:, P:H], "run1")
         q1_staged = keep.tile([P, P, PACK], BF16, name="q1_staged", align_bytes=64)
         stage_on_gpsimd(q1_staged[:], q_rest[:, :, 0:P])
-        q2_staged = keep.tile([P, P, PACK], BF16, name="q2_staged", align_bytes=64)
-        nc.scalar.copy(out=woven(q2_staged[:]), in_=rows(q_rest[:, :, P : 2 * P]))
+        q2_staged = stage[:, 0 : 2 * H].rearrange("p (n t) -> p n t", t=PACK)
+        nc.scalar.copy(out=woven(q2_staged), in_=rows(q_rest[:, :, P : 2 * P]))
         biased0 = keep.tile([P, N], F32, name="biased0")
         for r, bias in enumerate((kb_first[:], kb_listed[:, P:H])):
             cols = slice(r * P, (r + 1) * P)
@@ -134,7 +134,7 @@ def tile_attend_sddmm_kb_kernel(tc, qT, kT, kb, offs, out):
 
         quantize(second[:], "second")
         quantize(q1_staged[:], 1)
-        quantize(q2_staged[:], 2)
+        quantize(q2_staged, 2)
         acc = psum.tile([P, H], F32, name="acc0b", tag="acc0b")
         scores(acc[:], 0, "second")
         nc.vector.tensor_tensor(biased0[:, H:N], acc[:], kb_listed[:, H:N], add)

import concourse.mybir as mybir
from concourse.masks import make_identity

D, T, N, NQ = 512, 2048, 512, 384
P = 128
PACK = 4
H = N // 2
SHARE = 64

F32 = mybir.dt.float32
BF16 = mybir.dt.bfloat16
U32 = mybir.dt.uint32
U16 = mybir.dt.uint16
U8 = mybir.dt.uint8
FP8X4 = mybir.dt.float8_e4m3fn_x4

FLOPS = 2 * NQ * N * D
BYTES = 4 * (D * NQ + D * T + T + NQ * T) + 2 * P * (N // 16)


def tile_attend_sddmm_kb_kernel(tc, qT, kT, kb, offs, out):
    nc = tc.nc
    add = mybir.AluOpType.add
    copy = mybir.ActivationFunctionType.Copy
    with (
        tc.tile_pool(name="keep", bufs=1) as keep,
        tc.tile_pool(name="shared", bufs=1) as shared,
        tc.psum_pool(name="psum", bufs=1) as psum,
    ):
        kb_part = keep.tile([P, T // P], F32, name="kb_part")
        nc.sync.dma_start(out=kb_part[:], in_=kb[0].rearrange("(p c) -> p c", c=T // P))
        offsets = keep.tile([P, N // 16], U16, name="offsets")
        listed = [offsets[:, 0 : H // 16], offsets[:, H // 16 : N // 16]]

        k_rows = kT.rearrange("(p t) n -> p t n", t=PACK)
        planes = []
        for t in range(PACK):
            plane = keep.tile([P, T], F32, name=f"plane{t}", tag=f"plane{t}", align_bytes=256)
            nc.sync.dma_start(out=plane[:], in_=k_rows[:, t, :])
            planes.append(plane)
            if t == 0:
                nc.sync.dma_start(offsets[:], offs)
        q_rows = qT[0].rearrange("(p t) q -> p t q", t=PACK)
        q_first = keep.tile([P, PACK, P], F32, name="q_first", tag="q_first", align_bytes=256)
        nc.sync.dma_start(out=q_first[:], in_=q_rows[:, :, 0:P])
        q_rest = keep.tile([P, PACK, 2 * P], F32, name="q_rest", align_bytes=256)
        nc.sync.dma_start(out=q_rest[:], in_=q_rows[:, :, P:NQ])

        ident = keep.tile([P, P], F32, name="ident")
        make_identity(nc, ident[:])
        windows = [keep.tile([P, T], F32, name=f"window{m}", align_bytes=256) for m in range(3)]
        for cols in (slice(0, T // 2 + 1), slice(T // 2 + 1, T)):
            nc.vector.memset(windows[0][:, cols], 0.0)

        kb_pool = keep.tile([P, T], F32, name="kb_pool", tag="kb_pool", align_bytes=64)
        kb_view = kb_pool[:].rearrange("q (p c) -> q p c", c=T // P)
        for b in range(4):
            bank = psum.tile([P, 4, P], F32, name=f"bank{b}", tag=f"bank{b}")
            for j in range(4):
                c = 4 * b + j
                nc.tensor.transpose(bank[:, j, :], kb_part[:, c : c + 1].to_broadcast([P, P]), ident[:])
            nc.scalar.copy(out=kb_view[:, :, 4 * b : 4 * b + 4], in_=bank[:].rearrange("q c p -> q p c"))

        first = keep.tile([P, H, PACK], BF16, name="first", align_bytes=64)
        second = keep.tile([P, H, PACK], BF16, name="second", align_bytes=64)
        kb_listed = keep.tile([P, N], F32, name="kb_listed")
        nc.scalar.activation(kb_listed[:], kb_pool[:].indirect(offsets[:]), copy)
        kb_first = shared.tile([P, P], F32, name="kb_first", align_bytes=64, offset=0)
        nc.scalar.copy(out=kb_first[:], in_=kb_listed[:, 0:P])
        stage = keep.tile([P, 4 * H], BF16, name="stage", tag="kb_pool", align_bytes=64)
        second_rows = stage[:, 0 : 2 * H].rearrange("p (r n) -> p r n", n=H)
        q0_staged = stage[:, 2 * H : 4 * H].rearrange("p (n t) -> p n t", t=PACK)
        codes, scales = {}, {}
        scale_offsets = {"second": 0, 1: H, 2: H + P}

        def quantize(source, key):
            width = source.shape[1]
            tag = {"run0": "plane3", "run1": "q_first"}.get(key, f"codes_{key}")
            codes[key] = keep.tile([P, width], U32, name=f"codes_{key}", tag=tag, align_bytes=256)
            if key in scale_offsets:
                scales[key] = shared.tile([P, width], U8, name=f"scales_{key}", align_bytes=64, offset=scale_offsets[key])
            else:
                scales[key] = keep.tile([P, width], U8, name=f"scales_{key}", align_bytes=64)
            nc.vector.quantize_mx(
                out=codes[key][:].bitcast(FP8X4), scales=scales[key][:], in_=source.rearrange("p n t -> p (n t)")
            )

        def scores(acc, m, half):
            nc.tensor.matmul_mx(
                out=acc,
                lhsT=codes[m][:].bitcast(FP8X4),
                lhsT_scale=scales[m][:],
                rhs=codes[half][:].bitcast(FP8X4),
                rhs_scale=scales[half][:],
                start=True,
                stop=True,
            )

        def woven(target):
            return target.rearrange("p (c i) t -> p c t i", i=4)

        def rows(source):
            return source.rearrange("p t (c i) -> p c t i", i=4)

        def stage_on_gpsimd(target, source):
            nc.gpsimd.tensor_scalar(target, source.rearrange("p t q -> p q t"), 1.0, 0.0, mybir.AluOpType.mult, add)

        for t in range(PACK):
            nc.vector.tensor_copy(first[:, :, t], planes[t][:].indirect(listed[0]))
            if t < 2:
                nc.vector.tensor_copy(second[:, :, t], planes[t][:].indirect(listed[1]))
            else:
                nc.scalar.activation(second_rows[:, t - 2, :], planes[t][:].indirect(listed[1]), copy)
        for m in (1, 2):
            nc.vector.memset(windows[m][:], 0.0)

        nc.scalar.copy(out=woven(q0_staged[:, 0:SHARE]), in_=rows(q_first[:, :, 0:SHARE]))
        nc.vector.tensor_copy(woven(q0_staged[:, SHARE:P]), rows(q_first[:, :, SHARE:P]))
        nc.scalar.copy(out=woven(second[:, :, 2:4]), in_=rows(second_rows))
        quantize(first[:, 0:P], "run0")
        quantize(q0_staged, 0)
        quantize(first[:, P:H], "run1")
        q1_staged = keep.tile([P, P, PACK], BF16, name="q1_staged", align_bytes=64)
        stage_on_gpsimd(q1_staged[:], q_rest[:, :, 0:P])
        q2_staged = stage[:, 0 : 2 * H].rearrange("p (n t) -> p n t", t=PACK)
        nc.scalar.copy(out=woven(q2_staged), in_=rows(q_rest[:, :, P : 2 * P]))
        biased0 = keep.tile([P, N], F32, name="biased0")
        for r, bias in enumerate((kb_first[:], kb_listed[:, P:H])):
            cols = slice(r * P, (r + 1) * P)
            acc = psum.tile([P, P], F32, name=f"acc0a{r}", tag=f"acc0a{r}")
            scores(acc[:], 0, f"run{r}")
            nc.vector.tensor_tensor(biased0[:, cols], acc[:], bias, add)
        nc.scalar.activation(windows[0][:].indirect(listed[0]), biased0[:, 0:H], copy)

        quantize(second[:], "second")
        quantize(q1_staged[:], 1)
        quantize(q2_staged, 2)
        acc = psum.tile([P, H], F32, name="acc0b", tag="acc0b")
        scores(acc[:], 0, "second")
        nc.vector.tensor_tensor(biased0[:, H:N], acc[:], kb_listed[:, H:N], add)
        nc.scalar.activation(windows[0][:].indirect(listed[1]), biased0[:, H:N], copy)
        nc.sync.dma_start(out=out[0, 0:P, :], in_=windows[0][:])

        biased1 = keep.tile([P, N], F32, name="biased1")
        acc = psum.tile([P, N], F32, name="acc1", tag="acc1")
        scores(acc[:, 0:P], 1, "run0")
        scores(acc[:, P:H], 1, "run1")
        scores(acc[:, H:N], 1, "second")
        nc.vector.tensor_tensor(biased1[:], acc[:], kb_listed[:], add)
        biased2 = keep.tile([P, H], F32, name="biased2")
        acc = psum.tile([P, H], F32, name="acc2b", tag="bank0")
        scores(acc[:], 2, "second")
        nc.vector.tensor_tensor(biased2[:], acc[:], kb_listed[:, H:N], add)
        nc.vector.tensor_copy(windows[1][:].indirect(offsets[:]), biased1[:])
        nc.sync.dma_start(out=out[0, P : 2 * P, :], in_=windows[1][:])

        raw2 = keep.tile([P, H], F32, name="raw2")
        acc = psum.tile([P, H], F32, name="acc2a", tag="bank1")
        scores(acc[:, 0:P], 2, "run0")
        scores(acc[:, P:H], 2, "run1")
        nc.scalar.copy(out=raw2[:], in_=acc[:])
        nc.scalar.activation(windows[2][:].indirect(listed[1]), biased2[:], copy)
        nc.vector.tensor_tensor(windows[2][:].indirect(listed[0]), raw2[:], kb_listed[:, 0:H], add)
        nc.sync.dma_start(out=out[0, 2 * P : 3 * P, :], in_=windows[2][:])
